import numpy as np
import ml_dtypes


def mxq(x, axis, fmt="e4m3"):
    dtype, down = {"e4m3": (ml_dtypes.float8_e4m3fn, 7), "e5m2": (ml_dtypes.float8_e5m2, 14)}[fmt]
    v = np.moveaxis(np.asarray(x, np.float32).astype(ml_dtypes.bfloat16).astype(np.float64), axis, -1)
    blocks = v.reshape(v.shape[:-1] + (-1, 32))
    amax = np.abs(blocks).max(-1, keepdims=True)
    byte = np.maximum(np.where(amax > 0, np.frexp(amax)[1] - 1 + 127, 0) - down, 1)
    scale = np.exp2(byte - 127.0)
    codes = (blocks / scale).astype(np.float32).astype(dtype).astype(np.float64)
    return np.moveaxis((codes * scale).reshape(v.shape), -1, axis)


WIDE = False


def mx_kscale(k):
    if not WIDE:
        return np.ones(k)
    levels = np.array([10, -10, 5, -5, 0])
    if k % 512:
        return np.exp2(np.random.permutation(np.resize(levels, k // 32))).repeat(32)
    a = np.empty((k // 512, 16))
    for p in range(k // 512):
        a[p, :8] = np.random.permutation(np.resize(levels, 8))
        for g in range(8):
            far = levels[np.abs(levels - a[p, g]) >= 10]
            a[p, g + 8] = far[np.random.randint(len(far))]
    return np.exp2(a.ravel()).repeat(32)


def f64(x):
    return np.asarray(x).astype(np.float64)


def striped(idx):
    return np.tile(idx.reshape(-1, 16).T, (8, 1)).astype(np.uint16)


def unstriped(offs):
    return offs[:16].T.reshape(-1).astype(np.int64)


def sigmoid(v):
    return 1.0 / (1.0 + np.exp(-np.maximum(v, -700.0)))


K, T, E, H, N = 512, 512, 4, 512, 512
COUNTS = (128, 384, 256, 256)
STARTS = np.cumsum((0,) + COUNTS)


def by_expert(wq, xq):
    return np.concatenate([wq[e].T @ xq[:, STARTS[e]:STARTS[e + 1]] for e in range(E)], axis=1)


def setup_inputs():
    n = np.random.standard_normal
    s = mx_kscale(K)[:, None]
    u = mx_kscale(H)
    both = np.repeat(np.arange(E), COUNTS)
    pair = np.stack([both[:T], both[T:]])[:, np.random.permutation(T)]
    pair = np.where(np.random.rand(T) < 0.5, pair, pair[::-1])
    order = np.argsort(pair.reshape(-1), kind="stable")
    slot_token = order % T; pos = np.empty(2 * T, np.int64); pos[order] = np.arange(2 * T); pos = pos.reshape(2, T)
    g = np.random.uniform(0.2, 0.8, T)
    return {
        "xT": (n((K, T)) * s).astype(np.float32),
        "w1": (n((E, K, H)) / np.sqrt(K) / s[None]).astype(np.float32),
        "w3": (n((E, K, H)) / np.sqrt(K) / s[None] * u[None, None, :]).astype(np.float32),
        "w2": (n((E, H, N)) / np.sqrt(H) / u[None, :, None]).astype(np.float32),
        "gate": np.stack([np.tile(g, (N, 1)), np.tile(1.0 - g, (N, 1))]).astype(np.float32),
        "offs": striped(slot_token),
        "pos1": striped(pos[0]),
        "pos2": striped(pos[1]),
    }


def reference(xT, w1, w3, w2, gate, offs, pos1, pos2):
    idx = unstriped(offs)
    xq = mxq(f64(xT)[:, idx], 0, "e4m3")
    h = sigmoid(by_expert(mxq(f64(w1), 1, "e4m3"), xq))
    h = h * by_expert(mxq(f64(w3), 1, "e4m3"), xq)
    y = by_expert(mxq(f64(w2), 1, "e4m3"), mxq(h, 0, "e4m3"))
    return f64(gate[0]) * y[:, unstriped(pos1)] + f64(gate[1]) * y[:, unstriped(pos2)]

@@ -1,0 +1,167 @@
+from contextlib import ExitStack
+
+import concourse.mybir as mybir
+
+K, T, E, H, N = 512, 512, 4, 512, 512
+COUNTS = (128, 384, 256, 256)
+STARTS = (0, 128, 512, 768, 1024)
+S = 1024
+
+F32 = mybir.dt.float32
+BF16 = mybir.dt.bfloat16
+U32 = mybir.dt.uint32
+U16 = mybir.dt.uint16
+U8 = mybir.dt.uint8
+FP8X4 = mybir.dt.float8_e4m3fn_x4
+SIGMOID = mybir.ActivationFunctionType.Sigmoid
+MULT = mybir.AluOpType.mult
+ADD = mybir.AluOpType.add
+
+P = 128
+FLOPS = 2 * S * (2 * K * H + H * N)
+
+ORDER = (1, 2, 3, 0)
+S_SHARE_X = 3
+S_SHARE_1 = (5,6,6,8)
+S_SHARE_3 = (6,8,3,2)
+S_SHARE_2 = ((6,5,2,8), (8,4,2,5))
+Y_COPY = (("V", "S"), ("S", "S"), ("S", "S"), ("S", "S"))
+
+
+def tile_moe_rag_glu_sigmoid_kernel(tc, xT, w1, w3, w2, gate, offs, pos1, pos2, out):
+    nc = tc.nc
+    with ExitStack() as ctx:
+        lists = ctx.enter_context(tc.tile_pool(name="lists", bufs=1))
+        keep = ctx.enter_context(tc.tile_pool(name="keep", bufs=1))
+        grouped = ctx.enter_context(tc.tile_pool(name="grouped", bufs=4))
+        raws = ctx.enter_context(tc.tile_pool(name="raws", bufs=6))
+        work = ctx.enter_context(tc.tile_pool(name="work", bufs=3))
+        psum = ctx.enter_context(tc.psum_pool(name="psum", bufs=2))
+
+        offs_sb = lists.tile([P, S // 16], U16, name="offs_sb")
+        pos1_sb = lists.tile([P, T // 16], U16, name="pos1_sb")
+        pos2_sb = lists.tile([P, T // 16], U16, name="pos2_sb")
+
+        warm = keep.tile([P, 1], F32, name="warm")
+        nc.gpsimd.memset(warm[:], 0.0)
+        warm_out = keep.tile([P, 1], F32, name="warm_out")
+        nc.scalar.activation(out=warm_out[:], in_=warm[:], func=SIGMOID)
+
+        x_raw = keep.tile([P, 4, T], F32, name="x_raw")
+        nc.sync.dma_start(out=x_raw[:], in_=xT.rearrange("(p j) c -> p j c", j=4))
+        nc.sync.dma_start(offs_sb[:], offs)
+        w1_raw, w3_raw = {}, {}
+        for e in ORDER:
+            for src, lst, nm in ((w1, w1_raw, "w1"), (w3, w3_raw, "w3")):
+                t = raws.tile([P, 4, 512], F32, name="w_raw")
+                nc.sync.dma_start(out=t[:], in_=src[e].rearrange("(p j) c -> p j c", j=4))
+                lst[e] = t
+        nc.sync.dma_start(pos1_sb[:], pos1)
+        nc.sync.dma_start(pos2_sb[:], pos2)
+        w2_raw = {}
+        for hf in range(2):
+            for e in ORDER:
+                t = keep.tile([P, 4, 256], F32, name=f"w2_raw{hf}_{e}")
+                nc.sync.dma_start(out=t[:], in_=w2[e, :, hf * 256:(hf + 1) * 256].rearrange("(p j) c -> p j c", j=4))
+                w2_raw[hf, e] = t
+        gates = {}
+        for t in range(4):
+            for c in range(2):
+                gt = keep.tile([P, T], F32, name=f"gate{c}_{t}")
+                nc.sync.dma_start(out=gt[:], in_=gate[c, t * 128:(t + 1) * 128, :])
+                gates[c, t] = gt
+
+        def split_copy(dst, src, total, s_share):
+            if s_share:
+                nc.scalar.copy(out=dst[:, 0:s_share], in_=src[:, 0:s_share])
+            if s_share < total:
+                nc.vector.tensor_copy(out=dst[:, s_share:total], in_=src[:, s_share:total])
+
+        x_codes = keep.tile([P, T], U32, name="x_codes", align_bytes=64)
+        x_scales = keep.tile([P, T], U8, name="x_scales", align_bytes=64)
+        nc.gpsimd.memset(x_scales[:], 0)
+        xg = keep.tile([P, T, 4], BF16, name="xg", align_bytes=64)
+        split_copy(xg[:].rearrange("p (c i) j -> p c j i", i=4), x_raw[:].rearrange("p j (c i) -> p c j i", i=4), 128, 16 * S_SHARE_X)
+        nc.vector.quantize_mx(out=x_codes[:].bitcast(FP8X4), scales=x_scales[:], in_=xg[:].rearrange("p c j -> p (c j)"))
+
+        g_codes = keep.tile([P, S], U32, name="g_codes", align_bytes=64)
+        g_scales = keep.tile([P, S], U8, name="g_scales", align_bytes=64)
+
+        h_codes = keep.tile([P, S], U32, name="h_codes", align_bytes=64)
+        h_scales = keep.tile([P, S], U8, name="h_scales", align_bytes=64)
+
+        def first_weights(raw, e, nm, s_share):
+            wg = grouped.tile([P, 4, 128, 4], BF16, name="wg", align_bytes=64)
+            split_copy(wg[:].rearrange("p t m j -> p m j t"),
+                       raw[:].rearrange("p j (m t) -> p m j t", t=4), 128, s_share)
+            codes = keep.tile([P, 512], U32, name=f"{nm}_codes{e}", align_bytes=64)
+            scales = keep.tile([P, 512], U8, name=f"{nm}_scales{e}", align_bytes=64)
+            nc.vector.quantize_mx(out=codes[:].bitcast(FP8X4), scales=scales[:],
+                                  in_=wg[:].rearrange("p t m j -> p (t m j)"))
+            return codes, scales
+
+        for e in ORDER:
+            a, b = STARTS[e], STARTS[e + 1]
+            idx = offs_sb[:, a // 16:b // 16]
+            nc.vector.tensor_copy(out=g_codes[:, a:b], in_=x_codes[:].indirect(idx))
+            nc.vector.tensor_copy(out=g_scales[:, a:b], in_=x_scales[:].indirect(idx))
+            w1c, w1s = first_weights(w1_raw[e], e, "w1", 16 * S_SHARE_1[e])
+            w3c, w3s = first_weights(w3_raw[e], e, "w3", 16 * S_SHARE_3[e])
+            hb = keep.tile([P, b - a, 4], BF16, name=f"hb{e}", align_bytes=64)
+            for s0 in range(a, b, 128):
+                pa = psum.tile([P, 4, 128], F32, name="pa")
+                pb = psum.tile([P, 4, 128], F32, name="pb")
+                for acc, codes, scales in ((pa, w1c, w1s), (pb, w3c, w3s)):
+                    for t in range(4):
+                        cols = slice(t * 128, (t + 1) * 128)
+                        nc.tensor.matmul_mx(out=acc[:, t, :],
+                                            lhsT=codes[:, cols].bitcast(FP8X4), lhsT_scale=scales[:, cols],
+                                            rhs=g_codes[:, s0:s0 + 128].bitcast(FP8X4), rhs_scale=g_scales[:, s0:s0 + 128],
+                                            start=True, stop=True)
+                sig = work.tile([P, 128, 4], F32, name="sig")
+                nc.scalar.activation(out=sig[:], in_=pa[:].rearrange("p t n -> p n t"), func=SIGMOID)
+                nc.vector.tensor_tensor(out=hb[:, s0 - a:s0 - a + 128, :], in0=pb[:].rearrange("p t n -> p n t"), in1=sig[:], op=MULT)
+            q0 = a
+            while q0 < b:
+                w = 256 if b - q0 >= 256 else 128
+                nc.vector.quantize_mx(out=h_codes[:, q0:q0 + w].bitcast(FP8X4), scales=h_scales[:, q0:q0 + w],
+                                      in_=hb[:, q0 - a:q0 - a + w, :].rearrange("p n t -> p (n t)"))
+                q0 += w
+
+        w2c = {}
+        for hf in range(2):
+            for e in ORDER:
+                wg = grouped.tile([P, 256, 4], BF16, name="w2g", align_bytes=64)
+                split_copy(wg[:].rearrange("p (c i) j -> p c j i", i=4),
+                           w2_raw[hf, e][:].rearrange("p j (c i) -> p c j i", i=4), 64, 8 * S_SHARE_2[hf][e])
+                codes = keep.tile([P, 256], U32, name=f"w2_codes{hf}_{e}", align_bytes=64)
+                scales = keep.tile([P, 256], U8, name=f"w2_scales{hf}_{e}", align_bytes=64)
+                nc.vector.quantize_mx(out=codes[:].bitcast(FP8X4), scales=scales[:],
+                                      in_=wg[:].rearrange("p c j -> p (c j)"))
+                w2c[hf, e] = (codes, scales)
+        for hf in range(2):
+            for u in range(2):
+                t = 2 * hf + u
+                y = keep.tile([P, S], F32, name=f"y{t}")
+                for bank in range(2):
+                    py = psum.tile([P, 512], F32, name=f"py{bank}")
+                    for e, c0, c1 in (((0, 0, 128), (1, 128, 256), (1, 256, 512)), ((2, 512, 768), (3, 768, 1024)))[bank]:
+                        codes, scales = w2c[hf, e]
+                        cols = slice(u * 128, (u + 1) * 128)
+                        nc.tensor.matmul_mx(out=py[:, c0 - bank * 512:c1 - bank * 512],
+                                            lhsT=codes[:, cols].bitcast(FP8X4), lhsT_scale=scales[:, cols],
+                                            rhs=h_codes[:, c0:c1].bitcast(FP8X4), rhs_scale=h_scales[:, c0:c1],
+                                            start=True, stop=True)
+                    if Y_COPY[t][bank] == "S":
+                        nc.scalar.copy(out=y[:, bank * 512:(bank + 1) * 512], in_=py[:])
+                    else:
+                        nc.vector.tensor_copy(out=y[:, bank * 512:(bank + 1) * 512], in_=py[:])
+                r1 = work.tile([P, T], F32, name="r1")
+                r2 = work.tile([P, T], F32, name="r2")
+                nc.vector.tensor_tensor(out=r1[:], in0=y[:].indirect(pos1_sb[:]), in1=gates[0, t][:], op=MULT)
+                nc.vector.tensor_tensor(out=r2[:], in0=y[:].indirect(pos2_sb[:]), in1=gates[1, t][:], op=MULT)
+                pieces = 2 if t == 3 else 1
+                for i in range(pieces):
+                    cols = slice(i * T // pieces, (i + 1) * T // pieces)
+                    nc.vector.tensor_tensor(out=r1[:, cols], in0=r1[:, cols], in1=r2[:, cols], op=ADD)
+                    nc.sync.dma_start(out=out[t * 128:(t + 1) * 128, cols], in_=r1[:, cols])

@@ -21,11 +21,11 @@ P = 128
 FLOPS = 2 * S * (2 * K * H + H * N)
 
 ORDER = (1, 2, 3, 0)
-S_SHARE_X = 3
-S_SHARE_1 = (5,6,6,8)
-S_SHARE_3 = (6,8,3,2)
-S_SHARE_2 = ((6,5,2,8), (8,4,2,5))
-Y_COPY = (("V", "S"), ("S", "S"), ("S", "S"), ("S", "S"))
+S_SHARE_X = 1
+S_SHARE_1 = (5,5,5,5)
+S_SHARE_3 = (5,5,5,5)
+S_SHARE_2 = ((6,6,6,6), (4,4,4,4))
+Y_COPY = (("S", "S"), ("S", "S"), ("S", "S"), ("S", "S"))
 
 
 def tile_moe_rag_glu_sigmoid_kernel(tc, xT, w1, w3, w2, gate, offs, pos1, pos2, out):
@@ -34,7 +34,7 @@ def tile_moe_rag_glu_sigmoid_kernel(tc, xT, w1, w3, w2, gate, offs, pos1, pos2, 
         lists = ctx.enter_context(tc.tile_pool(name="lists", bufs=1))
         keep = ctx.enter_context(tc.tile_pool(name="keep", bufs=1))
         grouped = ctx.enter_context(tc.tile_pool(name="grouped", bufs=4))
-        raws = ctx.enter_context(tc.tile_pool(name="raws", bufs=6))
+        raws = ctx.enter_context(tc.tile_pool(name="raws", bufs=8))
         work = ctx.enter_context(tc.tile_pool(name="work", bufs=3))
         psum = ctx.enter_context(tc.psum_pool(name="psum", bufs=2))
 

@@ -3,7 +3,6 @@ from contextlib import ExitStack
 import concourse.mybir as mybir
 
 K, T, E, H, N = 512, 512, 4, 512, 512
-COUNTS = (128, 384, 256, 256)
 STARTS = (0, 128, 512, 768, 1024)
 S = 1024
 
@@ -12,6 +11,7 @@ BF16 = mybir.dt.bfloat16
 U32 = mybir.dt.uint32
 U16 = mybir.dt.uint16
 U8 = mybir.dt.uint8
+I32 = mybir.dt.int32
 FP8X4 = mybir.dt.float8_e4m3fn_x4
 SIGMOID = mybir.ActivationFunctionType.Sigmoid
 MULT = mybir.AluOpType.mult
@@ -20,11 +20,18 @@ ADD = mybir.AluOpType.add
 P = 128
 FLOPS = 2 * S * (2 * K * H + H * N)
 
-ORDER = (1, 2, 3, 0)
-S_SHARE_X = 1
-S_SHARE_1 = (5,5,5,5)
-S_SHARE_3 = (5,5,5,5)
-S_SHARE_2 = ((6,6,6,6), (4,4,4,4))
+
+GATHERS = ((0, 512), (512, 1024))
+WINDOW = 1024
+MERGED = (0, 0, 1, 0)
+STEPS = [["gath"],["w1",2],["w3",2],["w1",1],["w3",1],["comp",2],["w1",3],["w3",3],["comp",1],["w1",0],["w3",0],["comp",3],["comp",0],["w2",0,2],["w2",0,1],["w2",0,3],["w2",0,0],["w2",1,2],["w2",1,1],["w2",1,3],["w2",1,0],["y",0],["y",1],["y",2],["y",3]]
+ORDER = (2, 1, 3, 0)
+S_X = (0, 4)
+S_W1 = (2, 2, 8, 0)
+S_W3 = (4, 8, 8, 8)
+S_W2 = ((8, 0, 8, 8), (4, 8, 8, 0))
+Q2 = (((2, 1), (3, 0)), ((0,), (1,), (2,), (3,)))
+HQ = ((0, 4), (4, 8))
 Y_COPY = (("S", "S"), ("S", "S"), ("S", "S"), ("S", "S"))
 
 
@@ -33,10 +40,11 @@ def tile_moe_rag_glu_sigmoid_kernel(tc, xT, w1, w3, w2, gate, offs, pos1, pos2, 
     with ExitStack() as ctx:
         lists = ctx.enter_context(tc.tile_pool(name="lists", bufs=1))
         keep = ctx.enter_context(tc.tile_pool(name="keep", bufs=1))
-        grouped = ctx.enter_context(tc.tile_pool(name="grouped", bufs=4))
-        raws = ctx.enter_context(tc.tile_pool(name="raws", bufs=8))
+        grouped = ctx.enter_context(tc.tile_pool(name="grouped", bufs=3))
+        grouped2 = ctx.enter_context(tc.tile_pool(name="grouped2", bufs=4))
+        double = ctx.enter_context(tc.tile_pool(name="double", bufs=2))
         work = ctx.enter_context(tc.tile_pool(name="work", bufs=3))
-        psum = ctx.enter_context(tc.psum_pool(name="psum", bufs=2))
+        psum = ctx.enter_context(tc.psum_pool(name="psum", bufs=8))
 
         offs_sb = lists.tile([P, S // 16], U16, name="offs_sb")
         pos1_sb = lists.tile([P, T // 16], U16, name="pos1_sb")
@@ -47,29 +55,42 @@ def tile_moe_rag_glu_sigmoid_kernel(tc, xT, w1, w3, w2, gate, offs, pos1, pos2, 
         warm_out = keep.tile([P, 1], F32, name="warm_out")
         nc.scalar.activation(out=warm_out[:], in_=warm[:], func=SIGMOID)
 
-        x_raw = keep.tile([P, 4, T], F32, name="x_raw")
-        nc.sync.dma_start(out=x_raw[:], in_=xT.rearrange("(p j) c -> p j c", j=4))
+        def load_rows(src, cols, name):
+            t = keep.tile([P, 4, cols], F32, name=name, tag=name)
+            nc.sync.dma_start(out=t[:], in_=src.rearrange("(p j) c -> p j c", j=4))
+            return t
+
+        w1_raw, w3_raw, w2_raw, gates = {}, {}, {}, {}
+
+        def load_w2(hf):
+            for i, pair in enumerate((ORDER[:2], ORDER[2:])):
+                place = f"w{2 * i + 1}_raw{ORDER[0]}" if hf == 1 else f"w2_pair{i}"
+                raw = keep.tile([P, 2, 4, 256], F32, name=f"w2_raw{hf}_{i}", tag=place)
+                for k, e in enumerate(pair):
+                    nc.sync.dma_start(out=raw[:, k], in_=w2[e, :, hf * 256:(hf + 1) * 256].rearrange("(p j) c -> p j c", j=4))
+                    w2_raw[hf, e] = raw[:, k]
+
+        def load_gate(t):
+            if t % 2 == 0:
+                gates[t // 2] = keep.tile([P, 4, T], F32, name=f"gate{t // 2}", tag=f"w{t + 1}_raw{ORDER[1]}")
+            for c in range(2):
+                gt = gates[t // 2][:, 2 * (t % 2) + c, :]
+                nc.sync.dma_start(out=gt, in_=gate[c, t * 128:(t + 1) * 128, :])
+                gates[c, t] = gt
+
+        x_raw = []
+        for i in range(2):
+            x_raw.append(load_rows(xT[:, i * 256:(i + 1) * 256], 256, f"x_raw{i}"))
         nc.sync.dma_start(offs_sb[:], offs)
-        w1_raw, w3_raw = {}, {}
         for e in ORDER:
-            for src, lst, nm in ((w1, w1_raw, "w1"), (w3, w3_raw, "w3")):
-                t = raws.tile([P, 4, 512], F32, name="w_raw")
-                nc.sync.dma_start(out=t[:], in_=src[e].rearrange("(p j) c -> p j c", j=4))
-                lst[e] = t
+            w1_raw[e] = load_rows(w1[e], H, f"w1_raw{e}")
+            w3_raw[e] = load_rows(w3[e], H, f"w3_raw{e}")
         nc.sync.dma_start(pos1_sb[:], pos1)
         nc.sync.dma_start(pos2_sb[:], pos2)
-        w2_raw = {}
-        for hf in range(2):
-            for e in ORDER:
-                t = keep.tile([P, 4, 256], F32, name=f"w2_raw{hf}_{e}")
-                nc.sync.dma_start(out=t[:], in_=w2[e, :, hf * 256:(hf + 1) * 256].rearrange("(p j) c -> p j c", j=4))
-                w2_raw[hf, e] = t
-        gates = {}
-        for t in range(4):
-            for c in range(2):
-                gt = keep.tile([P, T], F32, name=f"gate{c}_{t}")
-                nc.sync.dma_start(out=gt[:], in_=gate[c, t * 128:(t + 1) * 128, :])
-                gates[c, t] = gt
+        load_w2(0)
+        load_w2(1)
+        for t in range(0, 4):
+            load_gate(t)
 
         def split_copy(dst, src, total, s_share):
             if s_share:
@@ -77,91 +98,145 @@ def tile_moe_rag_glu_sigmoid_kernel(tc, xT, w1, w3, w2, gate, offs, pos1, pos2, 
             if s_share < total:
                 nc.vector.tensor_copy(out=dst[:, s_share:total], in_=src[:, s_share:total])
 
-        x_codes = keep.tile([P, T], U32, name="x_codes", align_bytes=64)
-        x_scales = keep.tile([P, T], U8, name="x_scales", align_bytes=64)
+        x_words = keep.tile([P, WINDOW], I32, name="x_words", align_bytes=64)
+        nc.vector.memset(x_words[:, T:WINDOW], 0)
+        x_codes = x_words[:].bitcast(U32)
+        x_scales = keep.tile([P, WINDOW], U8, name="x_scales", align_bytes=64)
         nc.gpsimd.memset(x_scales[:], 0)
-        xg = keep.tile([P, T, 4], BF16, name="xg", align_bytes=64)
-        split_copy(xg[:].rearrange("p (c i) j -> p c j i", i=4), x_raw[:].rearrange("p j (c i) -> p c j i", i=4), 128, 16 * S_SHARE_X)
-        nc.vector.quantize_mx(out=x_codes[:].bitcast(FP8X4), scales=x_scales[:], in_=xg[:].rearrange("p c j -> p (c j)"))
-
         g_codes = keep.tile([P, S], U32, name="g_codes", align_bytes=64)
         g_scales = keep.tile([P, S], U8, name="g_scales", align_bytes=64)
-
+        h_bf = keep.tile([P, S, 4], BF16, name="h_bf", align_bytes=64)
         h_codes = keep.tile([P, S], U32, name="h_codes", align_bytes=64)
         h_scales = keep.tile([P, S], U8, name="h_scales", align_bytes=64)
 
-        def first_weights(raw, e, nm, s_share):
+        xg = keep.tile([P, T, 4], BF16, name="xg", align_bytes=64)
+        for i in range(2):
+            half = slice(i * 256, (i + 1) * 256)
+            split_copy(xg[:, half, :].rearrange("p (c i) j -> p c j i", i=4), x_raw[i][:].rearrange("p j (c i) -> p c j i", i=4), 64, 8 * S_X[i])
+            nc.vector.quantize_mx(out=x_words[:, half].bitcast(FP8X4), scales=x_scales[:, half], in_=xg[:, half, :].rearrange("p c j -> p (c j)"))
+
+        def gather(a, b):
+            idx = offs_sb[:, a // 16:b // 16]
+            nc.vector.tensor_copy(out=g_codes[:, a:b], in_=x_codes.indirect(idx))
+            nc.vector.tensor_copy(out=g_scales[:, a:b], in_=x_scales[:].indirect(idx))
+
+        pair_open = {}
+
+        def one_weight(raws, nm, e, s_share):
+            if MERGED[e]:
+                if e not in pair_open:
+                    wd = double.tile([P, 2, 4, 128, 4], BF16, name="wd", align_bytes=64)
+                    codes = keep.tile([P, 2, 512], U32, name=f"w13_{e}_codes", align_bytes=64)
+                    scales = keep.tile([P, 2, 512], U8, name=f"w13_{e}_scales", align_bytes=64)
+                    pair_open[e] = [wd, codes, scales, 0]
+                wd, codes, scales, n = pair_open[e]
+                i = 0 if nm == "w1" else 1
+                split_copy(wd[:, i].rearrange("p t m j -> p m j t"),
+                           raws[e][:].rearrange("p j (m t) -> p m j t", t=4), 128, 16 * s_share)
+                pair_open[e][3] = n + 1
+                if n == 1:
+                    nc.vector.quantize_mx(out=codes[:].rearrange("p w c -> p (w c)").bitcast(FP8X4),
+                                          scales=scales[:].rearrange("p w c -> p (w c)"),
+                                          in_=wd[:].rearrange("p w t m j -> p (w t m j)"))
+                return codes[:, i, :], scales[:, i, :]
             wg = grouped.tile([P, 4, 128, 4], BF16, name="wg", align_bytes=64)
             split_copy(wg[:].rearrange("p t m j -> p m j t"),
-                       raw[:].rearrange("p j (m t) -> p m j t", t=4), 128, s_share)
-            codes = keep.tile([P, 512], U32, name=f"{nm}_codes{e}", align_bytes=64)
-            scales = keep.tile([P, 512], U8, name=f"{nm}_scales{e}", align_bytes=64)
+                       raws[e][:].rearrange("p j (m t) -> p m j t", t=4), 128, 16 * s_share)
+            codes = keep.tile([P, 512], U32, name=f"{nm}_{e}_codes", align_bytes=64)
+            scales = keep.tile([P, 512], U8, name=f"{nm}_{e}_scales", align_bytes=64)
             nc.vector.quantize_mx(out=codes[:].bitcast(FP8X4), scales=scales[:],
                                   in_=wg[:].rearrange("p t m j -> p (t m j)"))
-            return codes, scales
+            return codes[:], scales[:]
 
-        for e in ORDER:
-            a, b = STARTS[e], STARTS[e + 1]
-            idx = offs_sb[:, a // 16:b // 16]
-            nc.vector.tensor_copy(out=g_codes[:, a:b], in_=x_codes[:].indirect(idx))
-            nc.vector.tensor_copy(out=g_scales[:, a:b], in_=x_scales[:].indirect(idx))
-            w1c, w1s = first_weights(w1_raw[e], e, "w1", 16 * S_SHARE_1[e])
-            w3c, w3s = first_weights(w3_raw[e], e, "w3", 16 * S_SHARE_3[e])
-            hb = keep.tile([P, b - a, 4], BF16, name=f"hb{e}", align_bytes=64)
-            for s0 in range(a, b, 128):
-                pa = psum.tile([P, 4, 128], F32, name="pa")
-                pb = psum.tile([P, 4, 128], F32, name="pb")
+        w2q = {}
+
+        w2_open = {}
+
+        def w2_step(hf, e):
+            for group in Q2[hf]:
+                if e not in group:
+                    continue
+                k = len(group)
+                if (hf, group) not in w2_open:
+                    wg = grouped2.tile([P, k, 256, 4], BF16, name="w2g", align_bytes=64)
+                    w2_open[hf, group] = [wg, 0]
+                wg = w2_open[hf, group][0]
+                split_copy(wg[:, group.index(e)].rearrange("p (c i) j -> p c j i", i=4),
+                           w2_raw[hf, e].rearrange("p j (c i) -> p c j i", i=4), 64, 8 * S_W2[hf][e])
+                w2_open[hf, group][1] += 1
+                if w2_open[hf, group][1] == k:
+                    codes = keep.tile([P, k * 256], U32, name=f"w2_codes{hf}_{group[0]}", align_bytes=64)
+                    scales = keep.tile([P, k * 256], U8, name=f"w2_scales{hf}_{group[0]}", align_bytes=64)
+                    nc.vector.quantize_mx(out=codes[:].bitcast(FP8X4), scales=scales[:],
+                                          in_=wg[:].rearrange("p k c j -> p (k c j)"))
+                    for i, g in enumerate(group):
+                        w2q[hf, g] = (codes, scales, i * 256)
+
+        done = set()
+
+        def hidden(e, w1c, w1s, w3c, w3s):
+            for chunk in range(STARTS[e] // 128, STARTS[e + 1] // 128):
+                slots = slice(chunk * 128, (chunk + 1) * 128)
+                pa = psum.tile([P, 4, 128], F32, name="pa", tag="bank")
+                pb = psum.tile([P, 4, 128], F32, name="pb", tag="bank")
                 for acc, codes, scales in ((pa, w1c, w1s), (pb, w3c, w3s)):
                     for t in range(4):
                         cols = slice(t * 128, (t + 1) * 128)
                         nc.tensor.matmul_mx(out=acc[:, t, :],
                                             lhsT=codes[:, cols].bitcast(FP8X4), lhsT_scale=scales[:, cols],
-                                            rhs=g_codes[:, s0:s0 + 128].bitcast(FP8X4), rhs_scale=g_scales[:, s0:s0 + 128],
+                                            rhs=g_codes[:, slots].bitcast(FP8X4), rhs_scale=g_scales[:, slots],
                                             start=True, stop=True)
                 sig = work.tile([P, 128, 4], F32, name="sig")
                 nc.scalar.activation(out=sig[:], in_=pa[:].rearrange("p t n -> p n t"), func=SIGMOID)
-                nc.vector.tensor_tensor(out=hb[:, s0 - a:s0 - a + 128, :], in0=pb[:].rearrange("p t n -> p n t"), in1=sig[:], op=MULT)
-            q0 = a
-            while q0 < b:
-                w = 256 if b - q0 >= 256 else 128
-                nc.vector.quantize_mx(out=h_codes[:, q0:q0 + w].bitcast(FP8X4), scales=h_scales[:, q0:q0 + w],
-                                      in_=hb[:, q0 - a:q0 - a + w, :].rearrange("p n t -> p (n t)"))
-                q0 += w
+                nc.vector.tensor_tensor(out=h_bf[:, slots, :], in0=pb[:].rearrange("p t n -> p n t"), in1=sig[:], op=MULT)
+                done.add(chunk)
+                for a, b in HQ:
+                    if a <= chunk < b and all(i in done for i in range(a, b)):
+                        hs = slice(a * 128, b * 128)
+                        nc.vector.quantize_mx(out=h_codes[:, hs].bitcast(FP8X4), scales=h_scales[:, hs],
+                                              in_=h_bf[:, hs, :].rearrange("p n t -> p (n t)"))
 
-        w2c = {}
-        for hf in range(2):
-            for e in ORDER:
-                wg = grouped.tile([P, 256, 4], BF16, name="w2g", align_bytes=64)
-                split_copy(wg[:].rearrange("p (c i) j -> p c j i", i=4),
-                           w2_raw[hf, e][:].rearrange("p j (c i) -> p c j i", i=4), 64, 8 * S_SHARE_2[hf][e])
-                codes = keep.tile([P, 256], U32, name=f"w2_codes{hf}_{e}", align_bytes=64)
-                scales = keep.tile([P, 256], U8, name=f"w2_scales{hf}_{e}", align_bytes=64)
-                nc.vector.quantize_mx(out=codes[:].bitcast(FP8X4), scales=scales[:],
-                                      in_=wg[:].rearrange("p c j -> p (c j)"))
-                w2c[hf, e] = (codes, scales)
-        for hf in range(2):
-            for u in range(2):
-                t = 2 * hf + u
-                y = keep.tile([P, S], F32, name=f"y{t}")
-                for bank in range(2):
-                    py = psum.tile([P, 512], F32, name=f"py{bank}")
-                    for e, c0, c1 in (((0, 0, 128), (1, 128, 256), (1, 256, 512)), ((2, 512, 768), (3, 768, 1024)))[bank]:
-                        codes, scales = w2c[hf, e]
-                        cols = slice(u * 128, (u + 1) * 128)
-                        nc.tensor.matmul_mx(out=py[:, c0 - bank * 512:c1 - bank * 512],
-                                            lhsT=codes[:, cols].bitcast(FP8X4), lhsT_scale=scales[:, cols],
-                                            rhs=h_codes[:, c0:c1].bitcast(FP8X4), rhs_scale=h_scales[:, c0:c1],
-                                            start=True, stop=True)
-                    if Y_COPY[t][bank] == "S":
-                        nc.scalar.copy(out=y[:, bank * 512:(bank + 1) * 512], in_=py[:])
-                    else:
-                        nc.vector.tensor_copy(out=y[:, bank * 512:(bank + 1) * 512], in_=py[:])
-                r1 = work.tile([P, T], F32, name="r1")
-                r2 = work.tile([P, T], F32, name="r2")
-                nc.vector.tensor_tensor(out=r1[:], in0=y[:].indirect(pos1_sb[:]), in1=gates[0, t][:], op=MULT)
-                nc.vector.tensor_tensor(out=r2[:], in0=y[:].indirect(pos2_sb[:]), in1=gates[1, t][:], op=MULT)
-                pieces = 2 if t == 3 else 1
-                for i in range(pieces):
-                    cols = slice(i * T // pieces, (i + 1) * T // pieces)
-                    nc.vector.tensor_tensor(out=r1[:, cols], in0=r1[:, cols], in1=r2[:, cols], op=ADD)
-                    nc.sync.dma_start(out=out[t * 128:(t + 1) * 128, cols], in_=r1[:, cols])
+
+        def outputs(t):
+            y = keep.tile([P, S], F32, name=f"y{t}")
+            for bank in range(2):
+                py = psum.tile([P, 512], F32, name=f"py{bank}", tag="bank")
+                for e, c0, c1 in (((0, 0, 128), (1, 128, 256), (1, 256, 512)), ((2, 512, 768), (3, 768, 1024)))[bank]:
+                    codes, scales, base = w2q[t // 2, e]
+                    cols = slice(base + (t % 2) * 128, base + (t % 2) * 128 + 128)
+                    nc.tensor.matmul_mx(out=py[:, c0 - bank * 512:c1 - bank * 512],
+                                        lhsT=codes[:, cols].bitcast(FP8X4), lhsT_scale=scales[:, cols],
+                                        rhs=h_codes[:, c0:c1].bitcast(FP8X4), rhs_scale=h_scales[:, c0:c1],
+                                        start=True, stop=True)
+                if Y_COPY[t][bank] == "S":
+                    nc.scalar.copy(out=y[:, bank * 512:(bank + 1) * 512], in_=py[:])
+                else:
+                    nc.vector.tensor_copy(out=y[:, bank * 512:(bank + 1) * 512], in_=py[:])
+            r1 = work.tile([P, T], F32, name="r1")
+            r2 = work.tile([P, T], F32, name="r2")
+            nc.vector.tensor_tensor(out=r1[:], in0=y[:].indirect(pos1_sb[:]), in1=gates[0, t], op=MULT)
+            nc.vector.tensor_tensor(out=r2[:], in0=y[:].indirect(pos2_sb[:]), in1=gates[1, t], op=MULT)
+            pieces = 2 if t == 3 else 1
+            for i in range(pieces):
+                cols = slice(i * T // pieces, (i + 1) * T // pieces)
+                nc.vector.tensor_tensor(out=r1[:, cols], in0=r1[:, cols], in1=r2[:, cols], op=ADD)
+                nc.sync.dma_start(out=out[t * 128:(t + 1) * 128, cols], in_=r1[:, cols])
+
+        weights = {}
+        for step in STEPS:
+            kind, args = step[0], step[1:]
+            if kind == "gath":
+                for a, b in GATHERS:
+                    gather(a, b)
+            elif kind == "g1":
+                gather(*GATHERS[args[0]])
+            elif kind == "w1":
+                weights["w1", args[0]] = one_weight(w1_raw, "w1", args[0], S_W1[args[0]])
+            elif kind == "w3":
+                weights["w3", args[0]] = one_weight(w3_raw, "w3", args[0], S_W3[args[0]])
+            elif kind == "comp":
+                hidden(args[0], *weights["w1", args[0]], *weights["w3", args[0]])
+            elif kind == "w2":
+                w2_step(args[0], args[1])
+            else:
+                outputs(args[0])

from contextlib import ExitStack

import concourse.mybir as mybir

K, T, E, H, N = 512, 512, 4, 512, 512
STARTS = (0, 128, 512, 768, 1024)
S = 1024

F32 = mybir.dt.float32
BF16 = mybir.dt.bfloat16
U32 = mybir.dt.uint32
U16 = mybir.dt.uint16
U8 = mybir.dt.uint8
I32 = mybir.dt.int32
FP8X4 = mybir.dt.float8_e4m3fn_x4
SIGMOID = mybir.ActivationFunctionType.Sigmoid
MULT = mybir.AluOpType.mult
ADD = mybir.AluOpType.add

P = 128
FLOPS = 2 * S * (2 * K * H + H * N)


GATHERS = ((0, 512), (512, 1024))
WINDOW = 1024
MERGED = (0, 0, 1, 0)
STEPS = [["gath"],["w1",2],["w3",2],["w1",1],["w3",1],["comp",2],["w1",3],["w3",3],["comp",1],["w1",0],["w3",0],["comp",3],["comp",0],["w2",0,2],["w2",0,1],["w2",0,3],["w2",0,0],["w2",1,2],["w2",1,1],["w2",1,3],["w2",1,0],["y",0],["y",1],["y",2],["y",3]]
ORDER = (2, 1, 3, 0)
S_X = (0, 4)
S_W1 = (2, 2, 8, 0)
S_W3 = (4, 8, 8, 8)
S_W2 = ((8, 0, 8, 8), (4, 8, 8, 0))
Q2 = (((2, 1), (3, 0)), ((0,), (1,), (2,), (3,)))
HQ = ((0, 4), (4, 8))
Y_COPY = (("S", "S"), ("S", "S"), ("S", "S"), ("S", "S"))


def tile_moe_rag_glu_sigmoid_kernel(tc, xT, w1, w3, w2, gate, offs, pos1, pos2, out):
    nc = tc.nc
    with ExitStack() as ctx:
        lists = ctx.enter_context(tc.tile_pool(name="lists", bufs=1))
        keep = ctx.enter_context(tc.tile_pool(name="keep", bufs=1))
        grouped = ctx.enter_context(tc.tile_pool(name="grouped", bufs=3))
        grouped2 = ctx.enter_context(tc.tile_pool(name="grouped2", bufs=4))
        double = ctx.enter_context(tc.tile_pool(name="double", bufs=2))
        work = ctx.enter_context(tc.tile_pool(name="work", bufs=3))
        psum = ctx.enter_context(tc.psum_pool(name="psum", bufs=8))

        offs_sb = lists.tile([P, S // 16], U16, name="offs_sb")
        pos1_sb = lists.tile([P, T // 16], U16, name="pos1_sb")
        pos2_sb = lists.tile([P, T // 16], U16, name="pos2_sb")

        warm = keep.tile([P, 1], F32, name="warm")
        nc.gpsimd.memset(warm[:], 0.0)
        warm_out = keep.tile([P, 1], F32, name="warm_out")
        nc.scalar.activation(out=warm_out[:], in_=warm[:], func=SIGMOID)

        def load_rows(src, cols, name):
            t = keep.tile([P, 4, cols], F32, name=name, tag=name)
            nc.sync.dma_start(out=t[:], in_=src.rearrange("(p j) c -> p j c", j=4))
            return t

        w1_raw, w3_raw, w2_raw, gates = {}, {}, {}, {}

        def load_w2(hf):
            for i, pair in enumerate((ORDER[:2], ORDER[2:])):
                place = f"w{2 * i + 1}_raw{ORDER[0]}" if hf == 1 else f"w2_pair{i}"
                raw = keep.tile([P, 2, 4, 256], F32, name=f"w2_raw{hf}_{i}", tag=place)
                for k, e in enumerate(pair):
                    nc.sync.dma_start(out=raw[:, k], in_=w2[e, :, hf * 256:(hf + 1) * 256].rearrange("(p j) c -> p j c", j=4))
                    w2_raw[hf, e] = raw[:, k]

        def load_gate(t):
            if t % 2 == 0:
                gates[t // 2] = keep.tile([P, 4, T], F32, name=f"gate{t // 2}", tag=f"w{t + 1}_raw{ORDER[1]}")
            for c in range(2):
                gt = gates[t // 2][:, 2 * (t % 2) + c, :]
                nc.sync.dma_start(out=gt, in_=gate[c, t * 128:(t + 1) * 128, :])
                gates[c, t] = gt

        x_raw = []
        for i in range(2):
            x_raw.append(load_rows(xT[:, i * 256:(i + 1) * 256], 256, f"x_raw{i}"))
        nc.sync.dma_start(offs_sb[:], offs)
        for e in ORDER:
            w1_raw[e] = load_rows(w1[e], H, f"w1_raw{e}")
            w3_raw[e] = load_rows(w3[e], H, f"w3_raw{e}")
        nc.sync.dma_start(pos1_sb[:], pos1)
        nc.sync.dma_start(pos2_sb[:], pos2)
        load_w2(0)
        load_w2(1)
        for t in range(0, 4):
            load_gate(t)

        def split_copy(dst, src, total, s_share):
            if s_share:
                nc.scalar.copy(out=dst[:, 0:s_share], in_=src[:, 0:s_share])
            if s_share < total:
                nc.vector.tensor_copy(out=dst[:, s_share:total], in_=src[:, s_share:total])

        x_words = keep.tile([P, WINDOW], I32, name="x_words", align_bytes=64)
        nc.vector.memset(x_words[:, T:WINDOW], 0)
        x_codes = x_words[:].bitcast(U32)
        x_scales = keep.tile([P, WINDOW], U8, name="x_scales", align_bytes=64)
        nc.gpsimd.memset(x_scales[:], 0)
        g_codes = keep.tile([P, S], U32, name="g_codes", align_bytes=64)
        g_scales = keep.tile([P, S], U8, name="g_scales", align_bytes=64)
        h_bf = keep.tile([P, S, 4], BF16, name="h_bf", align_bytes=64)
        h_codes = keep.tile([P, S], U32, name="h_codes", align_bytes=64)
        h_scales = keep.tile([P, S], U8, name="h_scales", align_bytes=64)

        xg = keep.tile([P, T, 4], BF16, name="xg", align_bytes=64)
        for i in range(2):
            half = slice(i * 256, (i + 1) * 256)
            split_copy(xg[:, half, :].rearrange("p (c i) j -> p c j i", i=4), x_raw[i][:].rearrange("p j (c i) -> p c j i", i=4), 64, 8 * S_X[i])
            nc.vector.quantize_mx(out=x_words[:, half].bitcast(FP8X4), scales=x_scales[:, half], in_=xg[:, half, :].rearrange("p c j -> p (c j)"))

        def gather(a, b):
            idx = offs_sb[:, a // 16:b // 16]
            nc.vector.tensor_copy(out=g_codes[:, a:b], in_=x_codes.indirect(idx))
            nc.vector.tensor_copy(out=g_scales[:, a:b], in_=x_scales[:].indirect(idx))

        pair_open = {}

        def one_weight(raws, nm, e, s_share):
            if MERGED[e]:
                if e not in pair_open:
                    wd = double.tile([P, 2, 4, 128, 4], BF16, name="wd", align_bytes=64)
                    codes = keep.tile([P, 2, 512], U32, name=f"w13_{e}_codes", align_bytes=64)
                    scales = keep.tile([P, 2, 512], U8, name=f"w13_{e}_scales", align_bytes=64)
                    pair_open[e] = [wd, codes, scales, 0]
                wd, codes, scales, n = pair_open[e]
                i = 0 if nm == "w1" else 1
                split_copy(wd[:, i].rearrange("p t m j -> p m j t"),
                           raws[e][:].rearrange("p j (m t) -> p m j t", t=4), 128, 16 * s_share)
                pair_open[e][3] = n + 1
                if n == 1:
                    nc.vector.quantize_mx(out=codes[:].rearrange("p w c -> p (w c)").bitcast(FP8X4),
                                          scales=scales[:].rearrange("p w c -> p (w c)"),
                                          in_=wd[:].rearrange("p w t m j -> p (w t m j)"))
                return codes[:, i, :], scales[:, i, :]
            wg = grouped.tile([P, 4, 128, 4], BF16, name="wg", align_bytes=64)
            split_copy(wg[:].rearrange("p t m j -> p m j t"),
                       raws[e][:].rearrange("p j (m t) -> p m j t", t=4), 128, 16 * s_share)
            codes = keep.tile([P, 512], U32, name=f"{nm}_{e}_codes", align_bytes=64)
            scales = keep.tile([P, 512], U8, name=f"{nm}_{e}_scales", align_bytes=64)
            nc.vector.quantize_mx(out=codes[:].bitcast(FP8X4), scales=scales[:],
                                  in_=wg[:].rearrange("p t m j -> p (t m j)"))
            return codes[:], scales[:]

        w2q = {}

        w2_open = {}

        def w2_step(hf, e):
            for group in Q2[hf]:
                if e not in group:
                    continue
                k = len(group)
                if (hf, group) not in w2_open:
                    wg = grouped2.tile([P, k, 256, 4], BF16, name="w2g", align_bytes=64)
                    w2_open[hf, group] = [wg, 0]
                wg = w2_open[hf, group][0]
                split_copy(wg[:, group.index(e)].rearrange("p (c i) j -> p c j i", i=4),
                           w2_raw[hf, e].rearrange("p j (c i) -> p c j i", i=4), 64, 8 * S_W2[hf][e])
                w2_open[hf, group][1] += 1
                if w2_open[hf, group][1] == k:
                    codes = keep.tile([P, k * 256], U32, name=f"w2_codes{hf}_{group[0]}", align_bytes=64)
                    scales = keep.tile([P, k * 256], U8, name=f"w2_scales{hf}_{group[0]}", align_bytes=64)
                    nc.vector.quantize_mx(out=codes[:].bitcast(FP8X4), scales=scales[:],
                                          in_=wg[:].rearrange("p k c j -> p (k c j)"))
                    for i, g in enumerate(group):
                        w2q[hf, g] = (codes, scales, i * 256)

        done = set()

        def hidden(e, w1c, w1s, w3c, w3s):
            for chunk in range(STARTS[e] // 128, STARTS[e + 1] // 128):
                slots = slice(chunk * 128, (chunk + 1) * 128)
                pa = psum.tile([P, 4, 128], F32, name="pa", tag="bank")
                pb = psum.tile([P, 4, 128], F32, name="pb", tag="bank")
                for acc, codes, scales in ((pa, w1c, w1s), (pb, w3c, w3s)):
                    for t in range(4):
                        cols = slice(t * 128, (t + 1) * 128)
                        nc.tensor.matmul_mx(out=acc[:, t, :],
                                            lhsT=codes[:, cols].bitcast(FP8X4), lhsT_scale=scales[:, cols],
                                            rhs=g_codes[:, slots].bitcast(FP8X4), rhs_scale=g_scales[:, slots],
                                            start=True, stop=True)
                sig = work.tile([P, 128, 4], F32, name="sig")
                nc.scalar.activation(out=sig[:], in_=pa[:].rearrange("p t n -> p n t"), func=SIGMOID)
                nc.vector.tensor_tensor(out=h_bf[:, slots, :], in0=pb[:].rearrange("p t n -> p n t"), in1=sig[:], op=MULT)
                done.add(chunk)
                for a, b in HQ:
                    if a <= chunk < b and all(i in done for i in range(a, b)):
                        hs = slice(a * 128, b * 128)
                        nc.vector.quantize_mx(out=h_codes[:, hs].bitcast(FP8X4), scales=h_scales[:, hs],
                                              in_=h_bf[:, hs, :].rearrange("p n t -> p (n t)"))


        def outputs(t):
            y = keep.tile([P, S], F32, name=f"y{t}")
            for bank in range(2):
                py = psum.tile([P, 512], F32, name=f"py{bank}", tag="bank")
                for e, c0, c1 in (((0, 0, 128), (1, 128, 256), (1, 256, 512)), ((2, 512, 768), (3, 768, 1024)))[bank]:
                    codes, scales, base = w2q[t // 2, e]
                    cols = slice(base + (t % 2) * 128, base + (t % 2) * 128 + 128)
                    nc.tensor.matmul_mx(out=py[:, c0 - bank * 512:c1 - bank * 512],
                                        lhsT=codes[:, cols].bitcast(FP8X4), lhsT_scale=scales[:, cols],
                                        rhs=h_codes[:, c0:c1].bitcast(FP8X4), rhs_scale=h_scales[:, c0:c1],
                                        start=True, stop=True)
                if Y_COPY[t][bank] == "S":
                    nc.scalar.copy(out=y[:, bank * 512:(bank + 1) * 512], in_=py[:])
                else:
                    nc.vector.tensor_copy(out=y[:, bank * 512:(bank + 1) * 512], in_=py[:])
            r1 = work.tile([P, T], F32, name="r1")
            r2 = work.tile([P, T], F32, name="r2")
            nc.vector.tensor_tensor(out=r1[:], in0=y[:].indirect(pos1_sb[:]), in1=gates[0, t], op=MULT)
            nc.vector.tensor_tensor(out=r2[:], in0=y[:].indirect(pos2_sb[:]), in1=gates[1, t], op=MULT)
            pieces = 2 if t == 3 else 1
            for i in range(pieces):
                cols = slice(i * T // pieces, (i + 1) * T // pieces)
                nc.vector.tensor_tensor(out=r1[:, cols], in0=r1[:, cols], in1=r2[:, cols], op=ADD)
                nc.sync.dma_start(out=out[t * 128:(t + 1) * 128, cols], in_=r1[:, cols])

        weights = {}
        for step in STEPS:
            kind, args = step[0], step[1:]
            if kind == "gath":
                for a, b in GATHERS:
                    gather(a, b)
            elif kind == "g1":
                gather(*GATHERS[args[0]])
            elif kind == "w1":
                weights["w1", args[0]] = one_weight(w1_raw, "w1", args[0], S_W1[args[0]])
            elif kind == "w3":
                weights["w3", args[0]] = one_weight(w3_raw, "w3", args[0], S_W3[args[0]])
            elif kind == "comp":
                hidden(args[0], *weights["w1", args[0]], *weights["w3", args[0]])
            elif kind == "w2":
                w2_step(args[0], args[1])
            else:
                outputs(args[0])
